import numpy as np
import ml_dtypes


def mxq(x, axis, fmt="e4m3"):
    dtype, down = {"e4m3": (ml_dtypes.float8_e4m3fn, 7), "e5m2": (ml_dtypes.float8_e5m2, 14)}[fmt]
    v = np.moveaxis(np.asarray(x, np.float32).astype(ml_dtypes.bfloat16).astype(np.float64), axis, -1)
    blocks = v.reshape(v.shape[:-1] + (-1, 32))
    amax = np.abs(blocks).max(-1, keepdims=True)
    byte = np.maximum(np.where(amax > 0, np.frexp(amax)[1] - 1 + 127, 0) - down, 1)
    scale = np.exp2(byte - 127.0)
    codes = (blocks / scale).astype(np.float32).astype(dtype).astype(np.float64)
    return np.moveaxis((codes * scale).reshape(v.shape), -1, axis)


WIDE = False


def mx_kscale(k):
    if not WIDE:
        return np.ones(k)
    levels = np.array([10, -10, 5, -5, 0])
    if k % 512:
        return np.exp2(np.random.permutation(np.resize(levels, k // 32))).repeat(32)
    a = np.empty((k // 512, 16))
    for p in range(k // 512):
        a[p, :8] = np.random.permutation(np.resize(levels, 8))
        for g in range(8):
            far = levels[np.abs(levels - a[p, g]) >= 10]
            a[p, g + 8] = far[np.random.randint(len(far))]
    return np.exp2(a.ravel()).repeat(32)


def f64(x):
    return np.asarray(x).astype(np.float64)


def striped8(idx):
    return np.asarray(idx).reshape(8, -1, 16).transpose(0, 2, 1).reshape(128, -1).astype(np.uint16)


def unstriped8(offs):
    return offs.reshape(8, 16, -1).transpose(0, 2, 1).reshape(8, -1).astype(np.int64)


def pick8(x, idx, run):
    r = np.arange(len(x))
    return x[r[:, None], idx[r % (8 * run) // run]]


E2M1 = np.array([0.0, 0.5, 1.0, 1.5, 2.0, 3.0, 4.0, 6.0, -0.0, -0.5, -1.0, -1.5, -2.0, -3.0, -4.0, -6.0])


def pack_weight(w, fmt):
    k, n = w.shape
    w = f64(np.asarray(w, np.float32).astype(ml_dtypes.bfloat16)).reshape(k // 32, 32, n)
    amax = np.abs(w).max(1)
    if fmt == "e4m3":
        byte = np.frexp(amax)[1] - 1 + 127 - 7
    else:
        mant, ex = np.frexp(amax / 6.0)
        byte = np.where(mant > 0.5, ex, ex - 1) + 127
    byte = np.clip(np.where(amax > 0, byte, 1), 1, 254)
    scaled = (w * np.exp2(127.0 - byte)[:, None, :]).reshape(k, n).astype(np.float32)
    by_word = np.ascontiguousarray(scaled.reshape(k // 512, 128, 4, n).transpose(0, 1, 3, 2))
    if fmt == "e4m3":
        words = by_word.astype(ml_dtypes.float8_e4m3fn).view(np.uint8)
    else:
        c = by_word.astype(ml_dtypes.float4_e2m1fn).view(np.uint8) & 0xF
        words = (c[..., 0::2] | (c[..., 1::2] << 4)).reshape(k // 512, 128, 2 * n)
    return np.ascontiguousarray(words), np.ascontiguousarray(byte.astype(np.uint8).reshape(k // 512, 16, n))


def unpack_weight(words, scales, fmt):
    g, _, n = scales.shape
    words = np.ascontiguousarray(words).reshape(g, 128, n, -1)
    if fmt == "e4m3":
        vals = words.view(ml_dtypes.float8_e4m3fn).astype(np.float64)
    else:
        nib = np.empty((g, 128, n, 4), np.uint8)
        nib[..., 0::2] = words & 0xF
        nib[..., 1::2] = words >> 4
        vals = E2M1[nib]
    vals = vals * np.repeat(np.exp2(scales.astype(np.float64) - 127.0), 8, axis=1)[..., None]
    return vals.transpose(0, 1, 3, 2).reshape(g * 512, n)


def sigmoid(v):
    return 1.0 / (1.0 + np.exp(-v))


D, K, T, U, I, Q = 512, 512, 1024, 1024, 512, 128


def setup_inputs():
    n = np.random.standard_normal
    idx = np.stack([np.random.permutation(T)[:I] for _ in range(8)])
    idx2 = np.stack([np.random.permutation(U)[:I] for _ in range(8)])
    idx3 = np.stack([np.random.permutation(U)[:I] for _ in range(8)])
    idx4 = np.stack([np.random.permutation(U)[:I] for _ in range(8)])
    fd = mx_kscale(D)
    fk = mx_kscale(K)
    wqp = pack_weight(n((D, K)) * 1.0 / np.sqrt(D) * fd[:, None] * fk, "e4m3")
    keysp = pack_weight(n((K, T)) * 1.0 / np.sqrt(K) / fk[:, None], "e2m1")
    notesp = pack_weight(n((D, U)) * 1.0 / np.sqrt(D) * fd[:, None], "e4m3")
    return {
        "states": (n((D, Q)) * 0.95 / fd[:, None]).astype(np.float32),
        "wq_words": wqp[0],
        "wq_scales": wqp[1],
        "keys_words": keysp[0],
        "keys_scales": keysp[1],
        "notes_words": notesp[0],
        "notes_scales": notesp[1],
        "thr": (np.random.uniform(-0.6, 0.6, (Q, 1))).astype(np.float32),
        "slope": (np.random.uniform(0.8, 2.0, (Q, 1))).astype(np.float32),
        "offs": striped8(idx),
        "offs2": striped8(idx2),
        "offs3": striped8(idx3),
        "offs4": striped8(idx4),
    }


def reference(states, wq_words, wq_scales, keys_words, keys_scales, notes_words, notes_scales, thr, slope, offs, offs2, offs3, offs4):
    idx = unstriped8(offs)
    idx2 = unstriped8(offs2)
    idx3 = unstriped8(offs3)
    idx4 = unstriped8(offs4)
    wqu = unpack_weight(wq_words, wq_scales, "e4m3")
    keysu = unpack_weight(keys_words, keys_scales, "e2m1")
    notesu = unpack_weight(notes_words, notes_scales, "e4m3")
    statesq = mxq(f64(states), 0, "e4m3")
    qv = wqu.T @ statesq
    qvq = mxq(qv, 0, "e4m3")
    a = qvq.T @ keysu
    b = statesq.T @ notesu
    f1 = np.zeros((Q, U))
    f1[np.arange(Q)[:, None], idx2[np.arange(Q) % 128 // 16]] = pick8(a, idx, 16)
    cc = b + f1
    s1 = sigmoid(pick8(cc, idx3, 16) * f64(slope) + f64(thr))
    f2 = np.zeros((Q, U))
    f2[np.arange(Q)[:, None], idx3[np.arange(Q) % 128 // 16]] = s1
    dd = cc - f2 * 2.0
    y = pick8(dd, idx4, 16)
    return y

from contextlib import ExitStack

import concourse.mybir as mybir

D, K, T, U, I, Q = 512, 512, 1024, 1024, 512, 128
FLOPS = 2 * Q * (D * K + K * T + D * U)

F32 = mybir.dt.float32
BF16 = mybir.dt.bfloat16
I32 = mybir.dt.int32
U32 = mybir.dt.uint32
U16 = mybir.dt.uint16
U8 = mybir.dt.uint8
FP8X4 = mybir.dt.float8_e4m3fn_x4
FP4X4 = mybir.dt.float4_e2m1fn_x4
ALU = mybir.AluOpType
ACT = mybir.ActivationFunctionType

P = 128
PACK = 4
BANK = 512
A_PIECE = 256
HALF = I // 2
HALF_COLS = HALF // 16


def load_scales(nc, plane, scales):
    rows = scales[0].bitcast(I32)
    nc.vector.memset(plane[:].bitcast(I32), 0)
    for g in range(4):
        nc.sync.dma_start(out=plane[32 * g : 32 * g + 4, :].bitcast(I32), in_=rows[4 * g : 4 * g + 4, :])


def load_scales_repeated(nc, plane, scales):
    rows = scales[0].bitcast(I32)
    for g in range(4):
        nc.scalar.dma_start(
            out=plane[32 * g : 32 * g + 32, :].bitcast(I32),
            in_=rows[4 * g : 4 * g + 4, :].unsqueeze(0).to_broadcast([8, 4, rows.shape[1]]),
        )


def tile_attend_throughgate_madeside_kernel(
    tc, states, wq_words, wq_scales, keys_words, keys_scales, notes_words, notes_scales,
    thr, slope, offs, offs2, offs3, offs4, out,
):
    nc = tc.nc
    with ExitStack() as ctx:
        lists = ctx.enter_context(tc.tile_pool(name="lists", bufs=1))
        sb = ctx.enter_context(tc.tile_pool(name="sb", bufs=1))
        psum = ctx.enter_context(tc.psum_pool(name="psum", bufs=1))

        wq_plane = sb.tile([P, K], U8, align_bytes=64)
        load_scales_repeated(nc, wq_plane, wq_scales)
        states_raw = sb.tile([P, PACK, Q], F32, align_bytes=64)
        nc.sync.dma_start(out=states_raw[:], in_=states.rearrange("(p j) q -> p j q", j=PACK))
        wq_raw = sb.tile([P, K], U32, align_bytes=64)
        nc.sync.dma_start(
            out=wq_raw[:].bitcast(I32), in_=wq_words[0].rearrange("p n t -> p (n t)").bitcast(I32)
        )
        keys = sb.tile([P, 2 * T], U8, align_bytes=64)
        nc.sync.dma_start(out=keys[:].bitcast(I32), in_=keys_words[0].bitcast(I32))
        keys_plane = sb.tile([P, T], U8, align_bytes=64)
        load_scales(nc, keys_plane, keys_scales)
        list_a = lists.tile([P, I // 16], U16)
        nc.sync.dma_start(list_a[:], offs)
        list_put = lists.tile([P, I // 16], U16)
        nc.sync.dma_start(list_put[:], offs2)
        notes = sb.tile([P, U], U32, align_bytes=64)
        nc.sync.dma_start(
            out=notes[:].bitcast(I32), in_=notes_words[0].rearrange("p n t -> p (n t)").bitcast(I32)
        )
        notes_plane = sb.tile([P, U], U8, align_bytes=64)
        load_scales(nc, notes_plane, notes_scales)
        list_gate = lists.tile([P, I // 16], U16)
        nc.sync.dma_start(list_gate[:], offs3)
        thr_col = sb.tile([P, 1], F32)
        nc.sync.dma_start(out=thr_col[:], in_=thr)
        slope_col = sb.tile([P, 1], F32)
        nc.sync.dma_start(out=slope_col[:], in_=slope)
        list_out = lists.tile([P, I // 16], U16)
        nc.sync.dma_start(list_out[:], offs4)

        f1 = sb.tile([P, U], F32)
        f2 = sb.tile([P, U], F32)
        nc.vector.memset(f1[:], 0.0)
        nc.vector.memset(f2[:], 0.0)

        wq_dealt_plane = sb.tile([P, K], U8, align_bytes=64)
        nc.vector.tensor_copy(
            out=wq_dealt_plane[:].rearrange("p (t m) -> p m t", t=PACK),
            in_=wq_plane[:].rearrange("p (m t) -> p m t", t=PACK),
        )

        states_bf = sb.tile([P, Q * PACK], BF16, align_bytes=64)
        nc.scalar.activation(
            out=states_bf[:].rearrange("p (c i t) -> p c t i", i=4, t=PACK),
            in_=states_raw[:].rearrange("p t (c i) -> p c t i", i=4),
            func=ACT.Copy,
        )
        wq_dealt = sb.tile([P, K], U32, align_bytes=64)
        nc.vector.tensor_copy(
            out=wq_dealt[:].bitcast(I32).rearrange("p (t c i) -> p c t i", t=PACK, i=4),
            in_=wq_raw[:].bitcast(I32).rearrange("p (c i t) -> p c t i", t=PACK, i=4),
        )
        states_codes = sb.tile([P, Q], U32, align_bytes=64)
        states_plane = sb.tile([P, Q], U8, align_bytes=64)
        nc.vector.quantize_mx(out=states_codes[:].bitcast(FP8X4), scales=states_plane[:], in_=states_bf[:])

        qv_ps = psum.tile([P, PACK, Q], F32)
        for t in range(PACK):
            cols = slice(t * P, (t + 1) * P)
            nc.tensor.matmul_mx(
                out=qv_ps[:, t, :],
                lhsT=wq_dealt[:, cols].bitcast(FP8X4), lhsT_scale=wq_dealt_plane[:, cols],
                rhs=states_codes[:].bitcast(FP8X4), rhs_scale=states_plane[:],
                start=True, stop=True,
            )
        qv_bf = sb.tile([P, Q * PACK], BF16, align_bytes=64)
        nc.scalar.copy(
            out=qv_bf[:].rearrange("p (q t) -> p q t", t=PACK),
            in_=qv_ps[:].rearrange("p t q -> p q t"),
        )
        qv_codes = sb.tile([P, Q], U32, align_bytes=64)
        qv_plane = sb.tile([P, Q], U8, align_bytes=64)
        nc.vector.quantize_mx(out=qv_codes[:].bitcast(FP8X4), scales=qv_plane[:], in_=qv_bf[:])

        a = sb.tile([P, T], F32)
        for j in range(T // A_PIECE):
            cols = slice(j * A_PIECE, (j + 1) * A_PIECE)
            a_ps = psum.tile([P, A_PIECE], F32, name=f"a_ps{j}")
            nc.tensor.matmul_mx(
                out=a_ps[:],
                lhsT=qv_codes[:].bitcast(FP8X4), lhsT_scale=qv_plane[:],
                rhs=keys[:, 2 * cols.start : 2 * cols.stop].bitcast(FP4X4), rhs_scale=keys_plane[:, cols],
                start=True, stop=True,
            )
            if j % 2 == 0:
                nc.vector.tensor_copy(out=a[:, cols], in_=a_ps[:])
            else:
                nc.scalar.copy(out=a[:, cols], in_=a_ps[:])

        b_banks = []
        for j in range(U // BANK):
            cols = slice(j * BANK, (j + 1) * BANK)
            b_ps = psum.tile([P, BANK], F32, name=f"b_ps{j}")
            nc.tensor.matmul_mx(
                out=b_ps[:],
                lhsT=states_codes[:].bitcast(FP8X4), lhsT_scale=states_plane[:],
                rhs=notes[:, cols].bitcast(FP8X4), rhs_scale=notes_plane[:, cols],
                start=True, stop=True,
            )
            b_banks.append(b_ps)

        picked = sb.tile([P, I], F32)
        nc.vector.tensor_copy(picked[:, :HALF], a[:].indirect(list_a[:, :HALF_COLS]))
        nc.scalar.activation(picked[:, HALF:], a[:].indirect(list_a[:, HALF_COLS:]), ACT.Copy)
        nc.vector.tensor_copy(f1[:].indirect(list_put[:]), picked[:])

        cc = sb.tile([P, U], F32)
        for j, b_ps in enumerate(b_banks):
            cols = slice(j * BANK, (j + 1) * BANK)
            nc.vector.tensor_tensor(cc[:, cols], b_ps[:], f1[:, cols], ALU.add)

        for h in range(2):
            entries = list_gate[:, h * HALF_COLS : (h + 1) * HALF_COLS]
            s1 = sb.tile([P, HALF], F32, name=f"s1_{h}")
            nc.scalar.activation(
                s1[:], cc[:].indirect(entries), ACT.Sigmoid, bias=thr_col[:], scale=slope_col[:]
            )
            nc.vector.tensor_copy(f2[:].indirect(entries), s1[:])

        dd = sb.tile([P, U], F32)
        nc.vector.scalar_tensor_tensor(dd[:], f2[:], -2.0, cc[:], ALU.mult, ALU.add)

        y0 = sb.tile([P, HALF], F32)
        nc.vector.tensor_copy(y0[:], dd[:].indirect(list_out[:, :HALF_COLS]))
        nc.sync.dma_start(out=out[:, :HALF], in_=y0[:])
        y1 = sb.tile([P, HALF], F32)
        nc.scalar.activation(y1[:], dd[:].indirect(list_out[:, HALF_COLS:]), ACT.Copy)
        nc.scalar.dma_start(out=out[:, HALF:], in_=y1[:])
